import numpy as np
CORES = [24,26,29,31,48,50,53,55]
N = 8
W = 512
def setup_inputs(rng):
    amp = 0.5 + 1.5 * rng.random((2, N, 128, 1), dtype=np.float32)
    return {"u": amp[0] * rng.standard_normal((N, 128, W), dtype=np.float32), "b": amp[1] * rng.standard_normal((N, 128, W), dtype=np.float32)}
def setup_inputs_big(rng):
    d = setup_inputs(rng)
    for k in ("u", "b"): d[k] = (d[k].astype(np.float32) * 1024.0).astype(d[k].dtype)
    return d
def setup_inputs_small(rng):
    d = setup_inputs(rng)
    for k in ("u", "b"): d[k] = (d[k].astype(np.float32) * (1 / 1024.0)).astype(d[k].dtype)
    return d
def setup_inputs_apart(rng):
    d = setup_inputs(rng)
    f = (10.0 ** rng.permutation(np.linspace(-1.5, 1.5, N))).astype(np.float32).reshape(N, 1, 1)
    for k in ("u", "b"): d[k] = (d[k].astype(np.float32) * f).astype(d[k].dtype)
    return d
def reference(u, b):
    g = np.concatenate(list(u.astype(np.float64)), axis=1); bb = np.concatenate(list(b.astype(np.float64)), axis=1)
    p = np.concatenate([g[:, -2:], g, g[:, :2]], axis=1)
    n = 0.125 * (p[:, :-4] + p[:, 1:-3] + p[:, 3:-1] + p[:, 4:]) + 0.5 * bb
    d = n - g
    s = np.stack([(d ** 2).mean(axis=1), np.abs(d).max(axis=1)], axis=1)
    return {"y": np.stack([n[:, W * r:W * r + W] for r in range(N)]).astype(np.float32), "s": np.broadcast_to(s.astype(np.float32), (N, 128, 2))}

@@ -1,0 +1,266 @@
+from concourse.bass import DstId, RemoteDMATransfer
+from concourse.mybir import AluOpType
+
+F32 = "float32"
+SCRATCH = {
+    "UX": ("sbuf", [128, 520], F32),
+    "Bb": ("sbuf", [128, 512], F32),
+    "PK": ("sbuf", [128, 6], F32),
+    "RL": ("sbuf", [128, 16], F32),
+    "S1": ("sbuf", [128, 512], F32),
+    "Q": ("sbuf", [128, 512], F32),
+    "E": ("sbuf", [128, 512], F32),
+    "SQ": ("sbuf", [128, 512], F32),
+    "ABR": ("sbuf", [128, 256], F32),
+    "Y": ("sbuf", [128, 512], F32),
+    "Wk": ("sbuf", [128, 1024], F32),
+    "Z2": ("sbuf", [128, 257], F32),
+    "D": ("dram", [128 * 257], F32),
+    "IB2": ("sbuf", [128, 256], F32),
+    "NI": ("sbuf", [128, 128], F32),
+    "LS": ("sbuf", [128, 16], F32),
+    "RS": ("sbuf", [128, 16], F32),
+    "FC": ("sbuf", [128, 2], F32),
+    "F": ("sbuf", [128, 2], F32),
+    "SS": ("sbuf", [128, 2], F32),
+    "PAL": ("psum", [128, 512], F32),
+    "PAR": ("psum", [128, 512], F32),
+    "PN": ("psum", [128, 512], F32),
+    "PC": ("psum", [128, 512], F32),
+    "PT": ("psum", [128, 512], F32),
+    "PS": ("psum", [128, 512], F32),
+    "PE": ("psum", [128, 512], F32),
+}
+SEMAPHORES = ["v", "ld_u", "ld_b", "ld_pk", "ld_d", "ld_i", "aL", "aR", "ae", "sm", "hl", "hr", "rl", "ls", "rs",
+              "snt", "st"]
+
+
+def rank_program(g, core, T, topo):
+    rank = T.rank_of(core)
+    if rank is None:
+        return
+    cores = list(T.cores)
+    n = len(cores)
+    S = T.sem
+    ADD, SUB, MUL, MAX = AluOpType.add, AluOpType.subtract, AluOpType.mult, AluOpType.max
+    vq, pe = g.vector, g.tensor
+    M8, P4 = T.IB2[:, 0:128], T.IB2[:, 128:256]
+
+    def bits(m):
+        return bin(m).count("1")
+
+    right, left = cores[(rank + 1) % n], cores[(rank - 1) % n]
+    for i in range(n):
+        assert topo.may_write(cores[i], cores[(i + 1) % n])
+
+    def via(i):
+        src, dst = cores[i], cores[(i - 1) % n]
+        if topo.may_write(src, dst):
+            return src
+        return [x for x in cores if x != src and topo.chip(x) == topo.chip(src) and topo.may_write(x, dst)][0]
+
+    here = [c for c in cores if topo.chip(c) == topo.chip(core)]
+    there = [c for c in cores if topo.chip(c) != topo.chip(core)]
+    assert 4 * len(here) == 16 and 4 * len(there) == 16 and len({topo.chip(c) for c in there}) == 1
+    slot = 4 * here.index(core)
+
+    def server(dst, group):
+        gws = [x for x in group if topo.may_write(x, dst)]
+        same = [x for x in gws if topo.die(x) == topo.die(dst)]
+        return (same or gws)[0]
+
+    serve = [d for d in there if server(d, here) == core]
+    gates = [x for x in here if any(server(d, here) == x for d in there)]
+
+    sent = [0]
+
+    def send(src_ap, dst_ap, dsts, sem):
+        m = topo.mask(core, dsts[0])
+        for d in dsts:
+            m &= topo.mask(core, d)
+        if len(dsts) == 1:
+            rid, pid, _ = topo.addr(dsts[0])
+            g.remote_dma(dst_ap, src_ap, sem, S.snt, pid, rid, m)
+        else:
+            ids = [DstId(rid=topo.addr(d)[0], pnc=topo.addr(d)[1]) for d in dsts]
+            g.remote_dma_fused([RemoteDMATransfer(dst_ids=ids, dma_engine_mask=m, remote_sem=sem, srcs=[src_ap],
+                                                  dsts=[dst_ap] * len(dsts), alu_op=0)], local_sem=S.snt)
+        sent[0] += bits(m)
+
+    nv = [0]
+
+    def dep():
+        if nv[0]:
+            vq.wait_ge(S.v, nv[0])
+
+    def done(ins):
+        ins.then_inc(S.v, 1)
+        nv[0] += 1
+        return nv[0]
+
+    def fill(ap, c):
+        dep()
+        return done(vq.memset(ap, c))
+
+    def tt(out, a, b, op):
+        dep()
+        return done(vq.tensor_tensor(out, a, b, op))
+
+    def cp(out, a):
+        dep()
+        return done(vq.tensor_copy(out, a))
+
+    wp = [0]
+
+    def wk(k):
+        a = wp[0]
+        wp[0] += k
+        return a
+
+    def W(o, k):
+        return T.Wk[:, o:o + k]
+
+    def halve(o, width, op, stop):
+        while width > stop:
+            width //= 2
+            o2 = wk(width)
+            tt(W(o2, width), W(o, width), W(o + width, width), op)
+            o = o2
+        return o
+
+    fill(T.Z2[:, :], 0.0)
+    fill(T.Z2[:, 0:1], -8.0)
+    n_z = fill(T.Z2[:, 128:129], 4.0)
+    fill(T.PC[:, 0:256], -1.0)
+    fill(T.PC[:, 256:512], 0.125)
+    fill(T.SQ[:, 0:2], 0.0)
+    fill(T.SQ[:, 510:512], 0.0)
+    fill(T.PT[:, 0:2], 0.0)
+    fill(T.ABR[:, 254:256], 0.0)
+    fill(T.LS[:, slot + 2:slot + 4], 0.0)
+    fill(T.FC[:, 0:1], 2.0 ** -18)
+    fill(T.FC[:, 1:2], 0.125)
+
+    g.sync.dma_start(T.UX[:, 6:518], T.u[:, :]).then_inc(S.ld_u, 16)
+    g.sync.dma_start(T.PK[:, 0:2], T.b[:, 510:512]).then_inc(S.ld_pk, 16)
+    g.sync.dma_start(T.PK[:, 2:6], T.u[:, 508:512]).then_inc(S.ld_pk, 16)
+    g.sync.dma_start(T.Bb[:, :], T.b[:, :]).then_inc(S.ld_b, 16)
+    g.scalar.wait_ge(S.v, n_z)
+    g.scalar.dma_start(T.D[:], T.Z2[:, :]).then_inc(S.ld_d, 16)
+    g.scalar.wait_ge(S.ld_d, 16)
+    g.scalar.dma_start(T.IB2[:, :], T.D[0:128 * 256]).then_inc(S.ld_i, 16)
+
+    vq.wait_ge(S.ld_u, 16)
+    tt(T.S1[:, 0:511], T.UX[:, 6:517], T.UX[:, 7:518], ADD)
+    tt(T.Q[:, 2:510], T.S1[:, 0:508], T.S1[:, 3:511], ADD)
+    vq.wait_ge(S.ld_i, 16)
+    tt(T.NI[:, :], T.PC[:, 256:384], M8, MUL)
+    vq.wait_ge(S.aL, 2)
+    tt(T.E[:, 2:256], T.PAL[:, 2:256], T.Q[:, 2:256], ADD)
+    tt(T.PN[:, 2:256], T.PC[:, 2:256], T.E[:, 2:256], MUL)
+    n_sql = tt(T.SQ[:, 2:256], T.PN[:, 2:256], T.E[:, 2:256], MUL)
+    tt(T.PT[:, 2:256], T.PN[:, 2:256], T.E[:, 2:256], MAX)
+    vq.wait_ge(S.aR, 2)
+    tt(T.E[:, 256:510], T.PAR[:, 0:254], T.Q[:, 256:510], ADD)
+    tt(T.PN[:, 256:510], T.PC[:, 0:254], T.E[:, 256:510], MUL)
+    n_sqr = tt(T.SQ[:, 256:510], T.PN[:, 256:510], T.E[:, 256:510], MUL)
+    tt(T.ABR[:, 0:254], T.PN[:, 256:510], T.E[:, 256:510], MAX)
+    t1, t2, t3 = wk(128), wk(64), wk(64)
+    tt(T.PT[:, 256:384], T.PT[:, 0:128], T.ABR[:, 0:128], MAX)
+    tt(W(t1, 128), T.PT[:, 128:256], T.ABR[:, 128:256], MAX)
+    tt(T.PT[:, 384:448], T.PT[:, 256:320], W(t1, 64), MAX)
+    tt(W(t2, 64), T.PT[:, 320:384], W(t1 + 64, 64), MAX)
+    tt(W(t3, 64), T.PT[:, 384:448], W(t2, 64), MAX)
+    m4 = halve(t3, 64, MAX, 4)
+    x = wk(64)
+    vq.wait_ge(S.sm, 7)
+    tt(W(x, 64), T.PS[:, 0:64], T.SQ[:, 448:512], SUB)
+    s4 = halve(x, 64, ADD, 4)
+    se, qe, ee, ne, sqe, s4b, m4b, m4c = wk(8), wk(4), wk(4), wk(4), wk(4), wk(4), wk(4), wk(4)
+    vq.wait_ge(S.hl, bits(topo.mask(left, core)))
+    tt(W(se, 7), T.UX[:, 2:9], T.UX[:, 3:10], ADD)
+    tt(W(qe, 4), W(se, 4), W(se + 3, 4), ADD)
+    vq.wait_ge(S.ae, 4)
+    tt(W(ee, 4), T.PE[:, 0:4], W(qe, 4), ADD)
+    tt(W(ne, 4), T.PC[:, 0:4], W(ee, 4), MUL)
+    tt(W(sqe, 4), W(ee, 4), W(ne, 4), MUL)
+    tt(W(s4b, 4), W(s4, 4), W(sqe, 4), SUB)
+    tt(W(m4b, 4), W(m4, 4), W(ee, 4), MAX)
+    tt(W(m4c, 4), W(m4b, 4), W(ne, 4), MAX)
+    s2 = halve(s4b, 4, ADD, 2)
+    m2 = halve(m4c, 4, MAX, 2)
+    tt(T.LS[:, slot:slot + 1], W(s2, 1), W(s2 + 1, 1), ADD)
+    n_part = tt(T.LS[:, slot + 1:slot + 2], W(m2, 1), W(m2 + 1, 1), MAX)
+
+    cp(T.E[:, 0:2], W(ee + 2, 2))
+    tt(T.PN[:, 0:256], T.PC[:, 256:512], T.E[:, 0:256], MUL)
+    tt(T.Y[:, 0:256], T.PN[:, 0:256], T.UX[:, 6:262], ADD)
+    sr, qr = wk(8), wk(2)
+    vq.wait_ge(S.hr, bits(topo.mask(via((rank + 1) % n), core)))
+    tt(W(sr, 5), T.UX[:, 514:519], T.UX[:, 515:520], ADD)
+    tt(W(qr, 2), W(sr, 2), W(sr + 3, 2), ADD)
+    tt(T.E[:, 510:512], T.PAR[:, 254:256], W(qr, 2), ADD)
+    tt(T.PN[:, 256:512], T.PC[:, 256:512], T.E[:, 256:512], MUL)
+    n_y = tt(T.Y[:, 256:512], T.PN[:, 256:512], T.UX[:, 262:518], ADD)
+
+    n_ls = sum(bits(topo.mask(c, core)) for c in here if c != core)
+    la, lm, la2, lm2 = wk(8), wk(8), wk(4), wk(4)
+    vq.wait_ge(S.ls, n_ls)
+    tt(W(la, 8), T.LS[:, 0:8], T.LS[:, 8:16], ADD)
+    tt(W(lm, 8), T.LS[:, 0:8], T.LS[:, 8:16], MAX)
+    tt(W(la2, 4), W(la, 4), W(la + 4, 4), ADD)
+    tt(W(lm2, 4), W(lm, 4), W(lm + 4, 4), MAX)
+    ra, rm, ra2, rm2 = wk(8), wk(8), wk(4), wk(4)
+    vq.wait_ge(S.rs, bits(topo.mask(server(core, there), core)))
+    tt(W(ra, 8), T.RS[:, 0:8], T.RS[:, 8:16], ADD)
+    tt(W(rm, 8), T.RS[:, 0:8], T.RS[:, 8:16], MAX)
+    tt(W(ra2, 4), W(ra, 4), W(ra + 4, 4), ADD)
+    tt(W(rm2, 4), W(rm, 4), W(rm + 4, 4), MAX)
+    tt(T.F[:, 0:1], W(ra2, 1), W(la2, 1), ADD)
+    tt(T.F[:, 1:2], W(rm2 + 1, 1), W(lm2 + 1, 1), MAX)
+    n_s = tt(T.SS[:, :], T.F[:, :], T.FC[:, :], MUL)
+
+    pe.wait_ge(S.ld_i, 16)
+    pe.wait_ge(S.ld_u, 16)
+    pe.matmul(T.PAL[:, 0:256], M8, T.UX[:, 6:262], True, False).then_inc(S.aL, 1)
+    pe.wait_ge(S.ld_b, 16)
+    pe.matmul(T.PAL[:, 0:256], P4, T.Bb[:, 0:256], False, True).then_inc(S.aL, 1)
+    pe.matmul(T.PAR[:, 0:256], M8, T.UX[:, 262:518], True, False).then_inc(S.aR, 1)
+    pe.matmul(T.PAR[:, 0:256], P4, T.Bb[:, 256:512], False, True).then_inc(S.aR, 1)
+    pe.matmul(T.PE[:, 2:4], M8, T.UX[:, 6:8], True, False).then_inc(S.ae, 1)
+    pe.matmul(T.PE[:, 2:4], P4, T.Bb[:, 0:2], False, True).then_inc(S.ae, 1)
+    pe.wait_ge(S.v, n_sql)
+    for k in range(7):
+        if k == 4:
+            pe.wait_ge(S.v, n_sqr)
+        pe.matmul(T.PS[:, 0:64], T.NI[:, :], T.SQ[:, 64 * k:64 * k + 64], k == 0, k == 6).then_inc(S.sm, 1)
+    pe.wait_ge(S.hl, bits(topo.mask(left, core)))
+    pe.matmul(T.PE[:, 0:2], M8, T.UX[:, 4:6], True, False).then_inc(S.ae, 1)
+    pe.matmul(T.PE[:, 0:2], P4, T.UX[:, 0:2], False, True).then_inc(S.ae, 1)
+
+    g.wait_ge(S.ld_pk, 32)
+    send(T.PK[:, 0:6], T.UX[:, 0:6], [right], S.hl)
+    g.wait_ge(S.ld_u, 16)
+    carrier = via(rank)
+    if carrier == core:
+        send(T.UX[:, 6:8], T.UX[:, 518:520], [left], S.hr)
+    else:
+        send(T.UX[:, 6:8], T.RL[:, 2 * rank:2 * rank + 2], [carrier], S.rl)
+    pass_on = [i for i in range(n) if i != rank and via(i) == core]
+    if pass_on:
+        g.wait_ge(S.rl, sum(bits(topo.mask(cores[i], core)) for i in pass_on))
+        for i in pass_on:
+            send(T.RL[:, 2 * i:2 * i + 2], T.UX[:, 518:520], [cores[(i - 1) % n]], S.hr)
+    g.wait_ge(S.v, n_part)
+    others = [c for c in gates if c != core] + [c for c in here if c != core and c not in gates]
+    send(T.LS[:, slot:slot + 4], T.LS[:, slot:slot + 4], others, S.ls)
+    if serve:
+        g.wait_ge(S.ls, n_ls)
+        send(T.LS[:, 0:16], T.RS[:, 0:16], serve, S.rs)
+    g.wait_ge(S.snt, sent[0])
+
+    g.sync.wait_ge(S.v, n_y)
+    g.sync.dma_start(T.y[:, :], T.Y[:, :]).then_inc(S.st, 16)
+    g.sync.wait_ge(S.v, n_s)
+    g.sync.dma_start(T.s[:, :], T.SS[:, :]).then_inc(S.st, 16)
+    g.sync.wait_ge(S.st, 32)

@@ -12,12 +12,13 @@ SCRATCH = {
     "E": ("sbuf", [128, 512], F32),
     "SQ": ("sbuf", [128, 512], F32),
     "ABR": ("sbuf", [128, 256], F32),
+    "TS": ("sbuf", [128, 128], F32),
+    "ONE": ("sbuf", [128, 1], F32),
     "Y": ("sbuf", [128, 512], F32),
     "Wk": ("sbuf", [128, 1024], F32),
     "Z2": ("sbuf", [128, 257], F32),
     "D": ("dram", [128 * 257], F32),
     "IB2": ("sbuf", [128, 256], F32),
-    "NI": ("sbuf", [128, 128], F32),
     "LS": ("sbuf", [128, 16], F32),
     "RS": ("sbuf", [128, 16], F32),
     "FC": ("sbuf", [128, 2], F32),
@@ -42,7 +43,7 @@ def rank_program(g, core, T, topo):
     cores = list(T.cores)
     n = len(cores)
     S = T.sem
-    ADD, SUB, MUL, MAX = AluOpType.add, AluOpType.subtract, AluOpType.mult, AluOpType.max
+    ADD, MUL, MAX = AluOpType.add, AluOpType.mult, AluOpType.max
     vq, pe = g.vector, g.tensor
     M8, P4 = T.IB2[:, 0:128], T.IB2[:, 128:256]
 
@@ -133,12 +134,9 @@ def rank_program(g, core, T, topo):
     n_z = fill(T.Z2[:, 128:129], 4.0)
     fill(T.PC[:, 0:256], -1.0)
     fill(T.PC[:, 256:512], 0.125)
-    fill(T.SQ[:, 0:2], 0.0)
-    fill(T.SQ[:, 510:512], 0.0)
-    fill(T.PT[:, 0:2], 0.0)
-    fill(T.ABR[:, 254:256], 0.0)
+    fill(T.ONE[:, :], 1.0)
     fill(T.LS[:, slot + 2:slot + 4], 0.0)
-    fill(T.FC[:, 0:1], 2.0 ** -18)
+    fill(T.FC[:, 0:1], 2.0 ** -21)
     fill(T.FC[:, 1:2], 0.125)
 
     g.sync.dma_start(T.UX[:, 6:518], T.u[:, :]).then_inc(S.ld_u, 16)
@@ -150,58 +148,47 @@ def rank_program(g, core, T, topo):
     g.scalar.wait_ge(S.ld_d, 16)
     g.scalar.dma_start(T.IB2[:, :], T.D[0:128 * 256]).then_inc(S.ld_i, 16)
 
+    n_hl = bits(topo.mask(left, core))
     vq.wait_ge(S.ld_u, 16)
     tt(T.S1[:, 0:511], T.UX[:, 6:517], T.UX[:, 7:518], ADD)
-    tt(T.Q[:, 2:510], T.S1[:, 0:508], T.S1[:, 3:511], ADD)
-    vq.wait_ge(S.ld_i, 16)
-    tt(T.NI[:, :], T.PC[:, 256:384], M8, MUL)
+    tt(T.Q[:, 0:508], T.S1[:, 0:508], T.S1[:, 3:511], ADD)
     vq.wait_ge(S.aL, 2)
-    tt(T.E[:, 2:256], T.PAL[:, 2:256], T.Q[:, 2:256], ADD)
-    tt(T.PN[:, 2:256], T.PC[:, 2:256], T.E[:, 2:256], MUL)
-    n_sql = tt(T.SQ[:, 2:256], T.PN[:, 2:256], T.E[:, 2:256], MUL)
-    tt(T.PT[:, 2:256], T.PN[:, 2:256], T.E[:, 2:256], MAX)
-    vq.wait_ge(S.aR, 2)
-    tt(T.E[:, 256:510], T.PAR[:, 0:254], T.Q[:, 256:510], ADD)
-    tt(T.PN[:, 256:510], T.PC[:, 0:254], T.E[:, 256:510], MUL)
-    n_sqr = tt(T.SQ[:, 256:510], T.PN[:, 256:510], T.E[:, 256:510], MUL)
-    tt(T.ABR[:, 0:254], T.PN[:, 256:510], T.E[:, 256:510], MAX)
-    t1, t2, t3 = wk(128), wk(64), wk(64)
-    tt(T.PT[:, 256:384], T.PT[:, 0:128], T.ABR[:, 0:128], MAX)
-    tt(W(t1, 128), T.PT[:, 128:256], T.ABR[:, 128:256], MAX)
-    tt(T.PT[:, 384:448], T.PT[:, 256:320], W(t1, 64), MAX)
-    tt(W(t2, 64), T.PT[:, 320:384], W(t1 + 64, 64), MAX)
-    tt(W(t3, 64), T.PT[:, 384:448], W(t2, 64), MAX)
-    m4 = halve(t3, 64, MAX, 4)
-    x = wk(64)
-    vq.wait_ge(S.sm, 7)
-    tt(W(x, 64), T.PS[:, 0:64], T.SQ[:, 448:512], SUB)
-    s4 = halve(x, 64, ADD, 4)
-    se, qe, ee, ne, sqe, s4b, m4b, m4c = wk(8), wk(4), wk(4), wk(4), wk(4), wk(4), wk(4), wk(4)
-    vq.wait_ge(S.hl, bits(topo.mask(left, core)))
+    tt(T.E[:, 0:256], T.PAL[:, 0:256], T.Q[:, 0:256], ADD)
+    tt(T.PN[:, 0:256], T.PC[:, 0:256], T.E[:, 0:256], MUL)
+    n_sql = tt(T.SQ[:, 0:256], T.PN[:, 0:256], T.E[:, 0:256], MUL)
+    tt(T.PT[:, 0:256], T.PN[:, 0:256], T.E[:, 0:256], MAX)
+    se = wk(8)
+    vq.wait_ge(S.hl, n_hl)
     tt(W(se, 7), T.UX[:, 2:9], T.UX[:, 3:10], ADD)
-    tt(W(qe, 4), W(se, 4), W(se + 3, 4), ADD)
-    vq.wait_ge(S.ae, 4)
-    tt(W(ee, 4), T.PE[:, 0:4], W(qe, 4), ADD)
-    tt(W(ne, 4), T.PC[:, 0:4], W(ee, 4), MUL)
-    tt(W(sqe, 4), W(ee, 4), W(ne, 4), MUL)
-    tt(W(s4b, 4), W(s4, 4), W(sqe, 4), SUB)
-    tt(W(m4b, 4), W(m4, 4), W(ee, 4), MAX)
-    tt(W(m4c, 4), W(m4b, 4), W(ne, 4), MAX)
-    s2 = halve(s4b, 4, ADD, 2)
-    m2 = halve(m4c, 4, MAX, 2)
-    tt(T.LS[:, slot:slot + 1], W(s2, 1), W(s2 + 1, 1), ADD)
-    n_part = tt(T.LS[:, slot + 1:slot + 2], W(m2, 1), W(m2 + 1, 1), MAX)
+    tt(T.Q[:, 508:512], W(se, 4), W(se + 3, 4), ADD)
+    vq.wait_ge(S.aR, 6)
+    tt(T.E[:, 256:512], T.PAR[:, 0:256], T.Q[:, 256:512], ADD)
+    tt(T.PN[:, 256:512], T.PC[:, 0:256], T.E[:, 256:512], MUL)
+    n_sqr = tt(T.SQ[:, 256:512], T.PN[:, 256:512], T.E[:, 256:512], MUL)
+    tt(T.ABR[:, 0:256], T.PN[:, 256:512], T.E[:, 256:512], MAX)
+    t1 = wk(256)
+    tt(W(t1, 256), T.PT[:, 0:256], T.ABR[:, 0:256], MAX)
+    m32 = halve(t1, 256, MAX, 32)
+    vq.wait_ge(S.sm, 4)
+    n_ts = cp(T.TS[:, :], T.PS[:, 0:128])
+    m2 = halve(m32, 32, MAX, 2)
+    tt(T.LS[:, slot + 1:slot + 2], W(m2, 1), W(m2 + 1, 1), MAX)
+    vq.wait_ge(S.sm, 5)
+    n_part = cp(T.LS[:, slot:slot + 1], T.PS[:, 128:129])
 
-    cp(T.E[:, 0:2], W(ee + 2, 2))
     tt(T.PN[:, 0:256], T.PC[:, 256:512], T.E[:, 0:256], MUL)
-    tt(T.Y[:, 0:256], T.PN[:, 0:256], T.UX[:, 6:262], ADD)
-    sr, qr = wk(8), wk(2)
+    tt(T.Y[:, 2:258], T.PN[:, 0:256], T.UX[:, 8:264], ADD)
+    tt(T.PN[:, 256:512], T.PC[:, 256:512], T.E[:, 256:512], MUL)
+    tt(T.Y[:, 258:510], T.PN[:, 256:508], T.UX[:, 264:516], ADD)
+    tt(T.Y[:, 0:2], T.PN[:, 510:512], T.UX[:, 6:8], ADD)
+    sr, qr, er = wk(8), wk(2), wk(2)
     vq.wait_ge(S.hr, bits(topo.mask(via((rank + 1) % n), core)))
     tt(W(sr, 5), T.UX[:, 514:519], T.UX[:, 515:520], ADD)
     tt(W(qr, 2), W(sr, 2), W(sr + 3, 2), ADD)
-    tt(T.E[:, 510:512], T.PAR[:, 254:256], W(qr, 2), ADD)
-    tt(T.PN[:, 256:512], T.PC[:, 256:512], T.E[:, 256:512], MUL)
-    n_y = tt(T.Y[:, 256:512], T.PN[:, 256:512], T.UX[:, 262:518], ADD)
+    vq.wait_ge(S.ae, 2)
+    tt(W(er, 2), T.PE[:, 0:2], W(qr, 2), ADD)
+    tt(T.PN[:, 0:2], T.PC[:, 256:258], W(er, 2), MUL)
+    n_y = tt(T.Y[:, 510:512], T.PN[:, 0:2], T.UX[:, 516:518], ADD)
 
     n_ls = sum(bits(topo.mask(c, core)) for c in here if c != core)
     la, lm, la2, lm2 = wk(8), wk(8), wk(4), wk(4)
@@ -222,21 +209,25 @@ def rank_program(g, core, T, topo):
 
     pe.wait_ge(S.ld_i, 16)
     pe.wait_ge(S.ld_u, 16)
-    pe.matmul(T.PAL[:, 0:256], M8, T.UX[:, 6:262], True, False).then_inc(S.aL, 1)
+    pe.matmul(T.PAL[:, 0:256], M8, T.UX[:, 8:264], True, False).then_inc(S.aL, 1)
     pe.wait_ge(S.ld_b, 16)
-    pe.matmul(T.PAL[:, 0:256], P4, T.Bb[:, 0:256], False, True).then_inc(S.aL, 1)
-    pe.matmul(T.PAR[:, 0:256], M8, T.UX[:, 262:518], True, False).then_inc(S.aR, 1)
-    pe.matmul(T.PAR[:, 0:256], P4, T.Bb[:, 256:512], False, True).then_inc(S.aR, 1)
-    pe.matmul(T.PE[:, 2:4], M8, T.UX[:, 6:8], True, False).then_inc(S.ae, 1)
-    pe.matmul(T.PE[:, 2:4], P4, T.Bb[:, 0:2], False, True).then_inc(S.ae, 1)
+    pe.matmul(T.PAL[:, 0:256], P4, T.Bb[:, 2:258], False, True).then_inc(S.aL, 1)
+    pe.matmul(T.PAR[:, 0:252], M8, T.UX[:, 264:516], True, False).then_inc(S.aR, 1)
+    pe.matmul(T.PAR[:, 0:252], P4, T.Bb[:, 258:510], False, True).then_inc(S.aR, 1)
+    pe.matmul(T.PAR[:, 254:256], M8, T.UX[:, 6:8], True, False).then_inc(S.aR, 1)
+    pe.matmul(T.PAR[:, 254:256], P4, T.Bb[:, 0:2], False, True).then_inc(S.aR, 1)
+    pe.wait_ge(S.hl, n_hl)
+    pe.matmul(T.PAR[:, 252:254], M8, T.UX[:, 4:6], True, False).then_inc(S.aR, 1)
+    pe.matmul(T.PAR[:, 252:254], P4, T.UX[:, 0:2], False, True).then_inc(S.aR, 1)
     pe.wait_ge(S.v, n_sql)
-    for k in range(7):
-        if k == 4:
+    for k in range(4):
+        if k == 2:
             pe.wait_ge(S.v, n_sqr)
-        pe.matmul(T.PS[:, 0:64], T.NI[:, :], T.SQ[:, 64 * k:64 * k + 64], k == 0, k == 6).then_inc(S.sm, 1)
-    pe.wait_ge(S.hl, bits(topo.mask(left, core)))
-    pe.matmul(T.PE[:, 0:2], M8, T.UX[:, 4:6], True, False).then_inc(S.ae, 1)
-    pe.matmul(T.PE[:, 0:2], P4, T.UX[:, 0:2], False, True).then_inc(S.ae, 1)
+        pe.matmul(T.PS[:, 0:128], T.SQ[:, 128 * k:128 * k + 128], M8, k == 0, k == 3).then_inc(S.sm, 1)
+    pe.wait_ge(S.v, n_ts)
+    pe.matmul(T.PS[:, 128:129], T.TS[:, :], T.ONE[:, :], True, True).then_inc(S.sm, 1)
+    pe.matmul(T.PE[:, 0:2], M8, T.UX[:, 516:518], True, False).then_inc(S.ae, 1)
+    pe.matmul(T.PE[:, 0:2], P4, T.Bb[:, 510:512], False, True).then_inc(S.ae, 1)
 
     g.wait_ge(S.ld_pk, 32)
     send(T.PK[:, 0:6], T.UX[:, 0:6], [right], S.hl)

@@ -32,7 +32,7 @@ SCRATCH = {
     "PS": ("psum", [128, 512], F32),
     "PE": ("psum", [128, 512], F32),
 }
-SEMAPHORES = ["v", "ld_u", "ld_b", "ld_pk", "ld_d", "ld_i", "aL", "aR", "ae", "sm", "hl", "hr", "rl", "ls", "rs",
+SEMAPHORES = ["v", "z", "ld_u", "ld_b", "ld_pk", "ld_d", "ld_i", "aL", "aR", "ae", "sm", "hl", "hr", "rl", "ls", "rs",
               "snt", "st"]
 
 
@@ -90,8 +90,8 @@ def rank_program(g, core, T, topo):
 
     nv = [0]
 
-    def dep():
-        if nv[0]:
+    def dep(new):
+        if new and nv[0]:
             vq.wait_ge(S.v, nv[0])
 
     def done(ins):
@@ -100,15 +100,14 @@ def rank_program(g, core, T, topo):
         return nv[0]
 
     def fill(ap, c):
-        dep()
         return done(vq.memset(ap, c))
 
-    def tt(out, a, b, op):
-        dep()
+    def tt(out, a, b, op, new=True):
+        dep(new)
         return done(vq.tensor_tensor(out, a, b, op))
 
-    def cp(out, a):
-        dep()
+    def cp(out, a, new=True):
+        dep(new)
         return done(vq.tensor_copy(out, a))
 
     wp = [0]
@@ -129,9 +128,10 @@ def rank_program(g, core, T, topo):
             o = o2
         return o
 
-    fill(T.Z2[:, :], 0.0)
-    fill(T.Z2[:, 0:1], -8.0)
-    n_z = fill(T.Z2[:, 128:129], 4.0)
+    vq.memset(T.Z2[:, 1:128], 0.0).then_inc(S.z, 1)
+    vq.memset(T.Z2[:, 129:257], 0.0).then_inc(S.z, 1)
+    vq.memset(T.Z2[:, 0:1], -8.0).then_inc(S.z, 1)
+    vq.memset(T.Z2[:, 128:129], 4.0).then_inc(S.z, 1)
     fill(T.PC[:, 0:256], -1.0)
     fill(T.PC[:, 256:512], 0.125)
     fill(T.ONE[:, :], 1.0)
@@ -140,50 +140,50 @@ def rank_program(g, core, T, topo):
     fill(T.FC[:, 1:2], 0.125)
 
     g.sync.dma_start(T.UX[:, 6:518], T.u[:, :]).then_inc(S.ld_u, 16)
-    g.sync.dma_start(T.PK[:, 0:2], T.b[:, 510:512]).then_inc(S.ld_pk, 16)
     g.sync.dma_start(T.PK[:, 2:6], T.u[:, 508:512]).then_inc(S.ld_pk, 16)
-    g.sync.dma_start(T.Bb[:, :], T.b[:, :]).then_inc(S.ld_b, 16)
-    g.scalar.wait_ge(S.v, n_z)
+    g.sync.dma_start(T.PK[:, 0:2], T.b[:, 510:512]).then_inc(S.ld_pk, 16)
+    g.scalar.dma_start(T.Bb[:, :], T.b[:, :]).then_inc(S.ld_b, 16)
+    g.scalar.wait_ge(S.z, 4)
     g.scalar.dma_start(T.D[:], T.Z2[:, :]).then_inc(S.ld_d, 16)
     g.scalar.wait_ge(S.ld_d, 16)
     g.scalar.dma_start(T.IB2[:, :], T.D[0:128 * 256]).then_inc(S.ld_i, 16)
 
     n_hl = bits(topo.mask(left, core))
+    se = wk(8)
     vq.wait_ge(S.ld_u, 16)
     tt(T.S1[:, 0:511], T.UX[:, 6:517], T.UX[:, 7:518], ADD)
     tt(T.Q[:, 0:508], T.S1[:, 0:508], T.S1[:, 3:511], ADD)
     vq.wait_ge(S.aL, 2)
     tt(T.E[:, 0:256], T.PAL[:, 0:256], T.Q[:, 0:256], ADD)
     tt(T.PN[:, 0:256], T.PC[:, 0:256], T.E[:, 0:256], MUL)
-    n_sql = tt(T.SQ[:, 0:256], T.PN[:, 0:256], T.E[:, 0:256], MUL)
-    tt(T.PT[:, 0:256], T.PN[:, 0:256], T.E[:, 0:256], MAX)
-    se = wk(8)
+    tt(T.SQ[:, 0:256], T.PN[:, 0:256], T.E[:, 0:256], MUL)
+    tt(T.PT[:, 0:256], T.PN[:, 0:256], T.E[:, 0:256], MAX, new=False)
     vq.wait_ge(S.hl, n_hl)
-    tt(W(se, 7), T.UX[:, 2:9], T.UX[:, 3:10], ADD)
+    n_sql = tt(W(se, 7), T.UX[:, 2:9], T.UX[:, 3:10], ADD, new=False)
     tt(T.Q[:, 508:512], W(se, 4), W(se + 3, 4), ADD)
     vq.wait_ge(S.aR, 6)
     tt(T.E[:, 256:512], T.PAR[:, 0:256], T.Q[:, 256:512], ADD)
     tt(T.PN[:, 256:512], T.PC[:, 0:256], T.E[:, 256:512], MUL)
-    n_sqr = tt(T.SQ[:, 256:512], T.PN[:, 256:512], T.E[:, 256:512], MUL)
-    tt(T.ABR[:, 0:256], T.PN[:, 256:512], T.E[:, 256:512], MAX)
+    tt(T.SQ[:, 256:512], T.PN[:, 256:512], T.E[:, 256:512], MUL)
+    n_sqr = tt(T.ABR[:, 0:256], T.PN[:, 256:512], T.E[:, 256:512], MAX, new=False)
     t1 = wk(256)
     tt(W(t1, 256), T.PT[:, 0:256], T.ABR[:, 0:256], MAX)
-    m32 = halve(t1, 256, MAX, 32)
+    m16 = halve(t1, 256, MAX, 16)
     vq.wait_ge(S.sm, 4)
-    n_ts = cp(T.TS[:, :], T.PS[:, 0:128])
-    m2 = halve(m32, 32, MAX, 2)
+    n_ts = cp(T.TS[:, :], T.PS[:, 0:128], new=False)
+    m2 = halve(m16, 16, MAX, 2)
     tt(T.LS[:, slot + 1:slot + 2], W(m2, 1), W(m2 + 1, 1), MAX)
     vq.wait_ge(S.sm, 5)
-    n_part = cp(T.LS[:, slot:slot + 1], T.PS[:, 128:129])
+    n_part = cp(T.LS[:, slot:slot + 1], T.PS[:, 128:129], new=False)
 
     tt(T.PN[:, 0:256], T.PC[:, 256:512], T.E[:, 0:256], MUL)
+    tt(T.PN[:, 256:512], T.PC[:, 256:512], T.E[:, 256:512], MUL, new=False)
     tt(T.Y[:, 2:258], T.PN[:, 0:256], T.UX[:, 8:264], ADD)
-    tt(T.PN[:, 256:512], T.PC[:, 256:512], T.E[:, 256:512], MUL)
-    tt(T.Y[:, 258:510], T.PN[:, 256:508], T.UX[:, 264:516], ADD)
-    tt(T.Y[:, 0:2], T.PN[:, 510:512], T.UX[:, 6:8], ADD)
+    tt(T.Y[:, 258:510], T.PN[:, 256:508], T.UX[:, 264:516], ADD, new=False)
+    tt(T.Y[:, 0:2], T.PN[:, 510:512], T.UX[:, 6:8], ADD, new=False)
     sr, qr, er = wk(8), wk(2), wk(2)
     vq.wait_ge(S.hr, bits(topo.mask(via((rank + 1) % n), core)))
-    tt(W(sr, 5), T.UX[:, 514:519], T.UX[:, 515:520], ADD)
+    tt(W(sr, 5), T.UX[:, 514:519], T.UX[:, 515:520], ADD, new=False)
     tt(W(qr, 2), W(sr, 2), W(sr + 3, 2), ADD)
     vq.wait_ge(S.ae, 2)
     tt(W(er, 2), T.PE[:, 0:2], W(qr, 2), ADD)
@@ -194,17 +194,17 @@ def rank_program(g, core, T, topo):
     la, lm, la2, lm2 = wk(8), wk(8), wk(4), wk(4)
     vq.wait_ge(S.ls, n_ls)
     tt(W(la, 8), T.LS[:, 0:8], T.LS[:, 8:16], ADD)
-    tt(W(lm, 8), T.LS[:, 0:8], T.LS[:, 8:16], MAX)
+    tt(W(lm, 8), T.LS[:, 0:8], T.LS[:, 8:16], MAX, new=False)
     tt(W(la2, 4), W(la, 4), W(la + 4, 4), ADD)
-    tt(W(lm2, 4), W(lm, 4), W(lm + 4, 4), MAX)
+    tt(W(lm2, 4), W(lm, 4), W(lm + 4, 4), MAX, new=False)
     ra, rm, ra2, rm2 = wk(8), wk(8), wk(4), wk(4)
     vq.wait_ge(S.rs, bits(topo.mask(server(core, there), core)))
     tt(W(ra, 8), T.RS[:, 0:8], T.RS[:, 8:16], ADD)
-    tt(W(rm, 8), T.RS[:, 0:8], T.RS[:, 8:16], MAX)
+    tt(W(rm, 8), T.RS[:, 0:8], T.RS[:, 8:16], MAX, new=False)
     tt(W(ra2, 4), W(ra, 4), W(ra + 4, 4), ADD)
-    tt(W(rm2, 4), W(rm, 4), W(rm + 4, 4), MAX)
+    tt(W(rm2, 4), W(rm, 4), W(rm + 4, 4), MAX, new=False)
     tt(T.F[:, 0:1], W(ra2, 1), W(la2, 1), ADD)
-    tt(T.F[:, 1:2], W(rm2 + 1, 1), W(lm2 + 1, 1), MAX)
+    tt(T.F[:, 1:2], W(rm2 + 1, 1), W(lm2 + 1, 1), MAX, new=False)
     n_s = tt(T.SS[:, :], T.F[:, :], T.FC[:, :], MUL)
 
     pe.wait_ge(S.ld_i, 16)

@@ -5,20 +5,21 @@ F32 = "float32"
 SCRATCH = {
     "UX": ("sbuf", [128, 520], F32),
     "Bb": ("sbuf", [128, 512], F32),
-    "PK": ("sbuf", [128, 6], F32),
     "RL": ("sbuf", [128, 16], F32),
     "S1": ("sbuf", [128, 512], F32),
     "Q": ("sbuf", [128, 512], F32),
     "E": ("sbuf", [128, 512], F32),
     "SQ": ("sbuf", [128, 512], F32),
-    "ABR": ("sbuf", [128, 256], F32),
     "TS": ("sbuf", [128, 128], F32),
     "ONE": ("sbuf", [128, 1], F32),
     "Y": ("sbuf", [128, 512], F32),
-    "Wk": ("sbuf", [128, 1024], F32),
-    "Z2": ("sbuf", [128, 257], F32),
-    "D": ("dram", [128 * 257], F32),
-    "IB2": ("sbuf", [128, 256], F32),
+    "Wk": ("sbuf", [128, 1280], F32),
+    "Za": ("sbuf", [128, 129], F32),
+    "Zb": ("sbuf", [128, 129], F32),
+    "Da": ("dram", [128 * 129], F32),
+    "Db": ("dram", [128 * 129], F32),
+    "M8": ("sbuf", [128, 128], F32),
+    "P4": ("sbuf", [128, 128], F32),
     "LS": ("sbuf", [128, 16], F32),
     "RS": ("sbuf", [128, 16], F32),
     "FC": ("sbuf", [128, 2], F32),
@@ -32,8 +33,8 @@ SCRATCH = {
     "PS": ("psum", [128, 512], F32),
     "PE": ("psum", [128, 512], F32),
 }
-SEMAPHORES = ["v", "z", "ld_u", "ld_b", "ld_pk", "ld_d", "ld_i", "aL", "aR", "ae", "sm", "hl", "hr", "rl", "ls", "rs",
-              "snt", "st"]
+SEMAPHORES = ["v", "za", "zb", "ld_u", "ld_b", "da", "db", "ia", "ib", "aL", "aR", "ae", "sm", "hu", "hb", "hr",
+              "rl", "ls", "rs", "snt", "st"]
 
 
 def rank_program(g, core, T, topo):
@@ -45,7 +46,7 @@ def rank_program(g, core, T, topo):
     S = T.sem
     ADD, MUL, MAX = AluOpType.add, AluOpType.mult, AluOpType.max
     vq, pe = g.vector, g.tensor
-    M8, P4 = T.IB2[:, 0:128], T.IB2[:, 128:256]
+    M8, P4 = T.M8[:, :], T.P4[:, :]
 
     def bits(m):
         return bin(m).count("1")
@@ -128,10 +129,10 @@ def rank_program(g, core, T, topo):
             o = o2
         return o
 
-    vq.memset(T.Z2[:, 1:128], 0.0).then_inc(S.z, 1)
-    vq.memset(T.Z2[:, 129:257], 0.0).then_inc(S.z, 1)
-    vq.memset(T.Z2[:, 0:1], -8.0).then_inc(S.z, 1)
-    vq.memset(T.Z2[:, 128:129], 4.0).then_inc(S.z, 1)
+    vq.memset(T.Za[:, 1:129], 0.0).then_inc(S.za, 1)
+    vq.memset(T.Za[:, 0:1], -8.0).then_inc(S.za, 1)
+    vq.memset(T.Zb[:, 1:129], 0.0).then_inc(S.zb, 1)
+    vq.memset(T.Zb[:, 0:1], 4.0).then_inc(S.zb, 1)
     fill(T.PC[:, 0:256], -1.0)
     fill(T.PC[:, 256:512], 0.125)
     fill(T.ONE[:, :], 1.0)
@@ -140,34 +141,36 @@ def rank_program(g, core, T, topo):
     fill(T.FC[:, 1:2], 0.125)
 
     g.sync.dma_start(T.UX[:, 6:518], T.u[:, :]).then_inc(S.ld_u, 16)
-    g.sync.dma_start(T.PK[:, 2:6], T.u[:, 508:512]).then_inc(S.ld_pk, 16)
-    g.sync.dma_start(T.PK[:, 0:2], T.b[:, 510:512]).then_inc(S.ld_pk, 16)
+    g.sync.wait_ge(S.zb, 2)
+    g.sync.dma_start(T.Db[:], T.Zb[:, :]).then_inc(S.db, 16)
+    g.sync.wait_ge(S.db, 16)
+    g.sync.dma_start(T.P4[:, :], T.Db[0:128 * 128]).then_inc(S.ib, 16)
     g.scalar.dma_start(T.Bb[:, :], T.b[:, :]).then_inc(S.ld_b, 16)
-    g.scalar.wait_ge(S.z, 4)
-    g.scalar.dma_start(T.D[:], T.Z2[:, :]).then_inc(S.ld_d, 16)
-    g.scalar.wait_ge(S.ld_d, 16)
-    g.scalar.dma_start(T.IB2[:, :], T.D[0:128 * 256]).then_inc(S.ld_i, 16)
+    g.scalar.wait_ge(S.za, 2)
+    g.scalar.dma_start(T.Da[:], T.Za[:, :]).then_inc(S.da, 16)
+    g.scalar.wait_ge(S.da, 16)
+    g.scalar.dma_start(T.M8[:, :], T.Da[0:128 * 128]).then_inc(S.ia, 16)
 
     n_hl = bits(topo.mask(left, core))
-    se = wk(8)
+    se, x1, t1 = wk(8), wk(256), wk(256)
     vq.wait_ge(S.ld_u, 16)
     tt(T.S1[:, 0:511], T.UX[:, 6:517], T.UX[:, 7:518], ADD)
     tt(T.Q[:, 0:508], T.S1[:, 0:508], T.S1[:, 3:511], ADD)
     vq.wait_ge(S.aL, 2)
-    tt(T.E[:, 0:256], T.PAL[:, 0:256], T.Q[:, 0:256], ADD)
+    tt(T.E[:, 0:256], T.PAL[:, 2:258], T.Q[:, 0:256], ADD)
+    vq.wait_ge(S.hu, n_hl)
+    tt(W(se, 7), T.UX[:, 2:9], T.UX[:, 3:10], ADD, new=False)
     tt(T.PN[:, 0:256], T.PC[:, 0:256], T.E[:, 0:256], MUL)
+    tt(T.Q[:, 508:512], W(se, 4), W(se + 3, 4), ADD, new=False)
     tt(T.SQ[:, 0:256], T.PN[:, 0:256], T.E[:, 0:256], MUL)
     tt(T.PT[:, 0:256], T.PN[:, 0:256], T.E[:, 0:256], MAX, new=False)
-    vq.wait_ge(S.hl, n_hl)
-    n_sql = tt(W(se, 7), T.UX[:, 2:9], T.UX[:, 3:10], ADD, new=False)
-    tt(T.Q[:, 508:512], W(se, 4), W(se + 3, 4), ADD)
-    vq.wait_ge(S.aR, 6)
-    tt(T.E[:, 256:512], T.PAR[:, 0:256], T.Q[:, 256:512], ADD)
+    tt(T.E[:, 510:512], T.PAL[:, 0:2], T.Q[:, 510:512], ADD, new=False)
+    vq.wait_ge(S.aR, 4)
+    n_sql = tt(T.E[:, 256:510], T.PAR[:, 0:254], T.Q[:, 256:510], ADD, new=False)
     tt(T.PN[:, 256:512], T.PC[:, 0:256], T.E[:, 256:512], MUL)
+    tt(W(x1, 256), T.PT[:, 0:256], T.E[:, 256:512], MAX, new=False)
     tt(T.SQ[:, 256:512], T.PN[:, 256:512], T.E[:, 256:512], MUL)
-    n_sqr = tt(T.ABR[:, 0:256], T.PN[:, 256:512], T.E[:, 256:512], MAX, new=False)
-    t1 = wk(256)
-    tt(W(t1, 256), T.PT[:, 0:256], T.ABR[:, 0:256], MAX)
+    n_sqr = tt(W(t1, 256), T.PN[:, 256:512], W(x1, 256), MAX, new=False)
     m16 = halve(t1, 256, MAX, 16)
     vq.wait_ge(S.sm, 4)
     n_ts = cp(T.TS[:, :], T.PS[:, 0:128], new=False)
@@ -207,17 +210,17 @@ def rank_program(g, core, T, topo):
     tt(T.F[:, 1:2], W(rm2 + 1, 1), W(lm2 + 1, 1), MAX, new=False)
     n_s = tt(T.SS[:, :], T.F[:, :], T.FC[:, :], MUL)
 
-    pe.wait_ge(S.ld_i, 16)
+    pe.wait_ge(S.ia, 16)
     pe.wait_ge(S.ld_u, 16)
-    pe.matmul(T.PAL[:, 0:256], M8, T.UX[:, 8:264], True, False).then_inc(S.aL, 1)
+    pe.matmul(T.PAL[:, 0:258], M8, T.UX[:, 6:264], True, False).then_inc(S.aL, 1)
+    pe.wait_ge(S.ib, 16)
     pe.wait_ge(S.ld_b, 16)
-    pe.matmul(T.PAL[:, 0:256], P4, T.Bb[:, 2:258], False, True).then_inc(S.aL, 1)
+    pe.matmul(T.PAL[:, 0:258], P4, T.Bb[:, 0:258], False, True).then_inc(S.aL, 1)
     pe.matmul(T.PAR[:, 0:252], M8, T.UX[:, 264:516], True, False).then_inc(S.aR, 1)
     pe.matmul(T.PAR[:, 0:252], P4, T.Bb[:, 258:510], False, True).then_inc(S.aR, 1)
-    pe.matmul(T.PAR[:, 254:256], M8, T.UX[:, 6:8], True, False).then_inc(S.aR, 1)
-    pe.matmul(T.PAR[:, 254:256], P4, T.Bb[:, 0:2], False, True).then_inc(S.aR, 1)
-    pe.wait_ge(S.hl, n_hl)
+    pe.wait_ge(S.hu, n_hl)
     pe.matmul(T.PAR[:, 252:254], M8, T.UX[:, 4:6], True, False).then_inc(S.aR, 1)
+    pe.wait_ge(S.hb, n_hl)
     pe.matmul(T.PAR[:, 252:254], P4, T.UX[:, 0:2], False, True).then_inc(S.aR, 1)
     pe.wait_ge(S.v, n_sql)
     for k in range(4):
@@ -229,9 +232,10 @@ def rank_program(g, core, T, topo):
     pe.matmul(T.PE[:, 0:2], M8, T.UX[:, 516:518], True, False).then_inc(S.ae, 1)
     pe.matmul(T.PE[:, 0:2], P4, T.Bb[:, 510:512], False, True).then_inc(S.ae, 1)
 
-    g.wait_ge(S.ld_pk, 32)
-    send(T.PK[:, 0:6], T.UX[:, 0:6], [right], S.hl)
     g.wait_ge(S.ld_u, 16)
+    send(T.UX[:, 514:518], T.UX[:, 2:6], [right], S.hu)
+    g.wait_ge(S.ld_b, 16)
+    send(T.Bb[:, 510:512], T.UX[:, 0:2], [right], S.hb)
     carrier = via(rank)
     if carrier == core:
         send(T.UX[:, 6:8], T.UX[:, 518:520], [left], S.hr)

@@ -1,40 +1,34 @@
 from concourse.bass import DstId, RemoteDMATransfer
-from concourse.mybir import AluOpType
+from concourse.mybir import AluOpType, AxisListType, ActivationFunctionType
 
 F32 = "float32"
 SCRATCH = {
     "UX": ("sbuf", [128, 520], F32),
-    "Bb": ("sbuf", [128, 512], F32),
+    "BX": ("sbuf", [128, 516], F32),
     "RL": ("sbuf", [128, 16], F32),
-    "S1": ("sbuf", [128, 512], F32),
+    "Z": ("sbuf", [128, 516], F32),
     "Q": ("sbuf", [128, 512], F32),
+    "G": ("sbuf", [128, 512], F32),
     "E": ("sbuf", [128, 512], F32),
-    "SQ": ("sbuf", [128, 512], F32),
-    "TS": ("sbuf", [128, 128], F32),
-    "ONE": ("sbuf", [128, 1], F32),
+    "J": ("sbuf", [128, 512], F32),
+    "J2": ("sbuf", [128, 32], F32),
     "Y": ("sbuf", [128, 512], F32),
-    "Wk": ("sbuf", [128, 1280], F32),
-    "Za": ("sbuf", [128, 129], F32),
-    "Zb": ("sbuf", [128, 129], F32),
-    "Da": ("dram", [128 * 129], F32),
-    "Db": ("dram", [128 * 129], F32),
-    "M8": ("sbuf", [128, 128], F32),
-    "P4": ("sbuf", [128, 128], F32),
-    "LS": ("sbuf", [128, 16], F32),
-    "RS": ("sbuf", [128, 16], F32),
-    "FC": ("sbuf", [128, 2], F32),
-    "F": ("sbuf", [128, 2], F32),
-    "SS": ("sbuf", [128, 2], F32),
-    "PAL": ("psum", [128, 512], F32),
-    "PAR": ("psum", [128, 512], F32),
-    "PN": ("psum", [128, 512], F32),
-    "PC": ("psum", [128, 512], F32),
-    "PT": ("psum", [128, 512], F32),
-    "PS": ("psum", [128, 512], F32),
-    "PE": ("psum", [128, 512], F32),
+    "Y01": ("sbuf", [128, 2], F32),
+    "YT": ("sbuf", [128, 2], F32),
+    "A1": ("sbuf", [128, 4], F32),
+    "A2": ("sbuf", [128, 4], F32),
+    "GT": ("sbuf", [128, 2], F32),
+    "ZT": ("sbuf", [128, 2], F32),
+    "ST": ("sbuf", [128, 64], F32),
+    "CF": ("sbuf", [128, 32], F32),
+    "FB": ("sbuf", [128, 64], F32),
+    "PU1": ("psum", [128, 512], F32),
+    "PU2": ("psum", [128, 512], F32),
+    "PB1": ("psum", [128, 512], F32),
+    "PB2": ("psum", [128, 512], F32),
+    "PSm": ("psum", [128, 512], F32),
 }
-SEMAPHORES = ["v", "za", "zb", "ld_u", "ld_b", "da", "db", "ia", "ib", "aL", "aR", "ae", "sm", "hu", "hb", "hr",
-              "rl", "ls", "rs", "snt", "st"]
+SEMAPHORES = ["v", "a", "ld_u1", "ld_u2", "ld_b1", "ld_b2", "hu", "hb", "hr", "rl", "ls", "rs", "snt", "st"]
 
 
 def rank_program(g, core, T, topo):
@@ -45,8 +39,9 @@ def rank_program(g, core, T, topo):
     n = len(cores)
     S = T.sem
     ADD, MUL, MAX = AluOpType.add, AluOpType.mult, AluOpType.max
-    vq, pe = g.vector, g.tensor
-    M8, P4 = T.M8[:, :], T.P4[:, :]
+    COPY, SQUARE = ActivationFunctionType.Copy, ActivationFunctionType.Square
+    vq, aq = g.vector, g.scalar
+    UX, BX, Z, Q, G, E, ST = T.UX, T.BX, T.Z, T.Q, T.G, T.E, T.ST
 
     def bits(m):
         return bin(m).count("1")
@@ -63,8 +58,8 @@ def rank_program(g, core, T, topo):
 
     here = [c for c in cores if topo.chip(c) == topo.chip(core)]
     there = [c for c in cores if topo.chip(c) != topo.chip(core)]
-    assert 4 * len(here) == 16 and 4 * len(there) == 16 and len({topo.chip(c) for c in there}) == 1
-    slot = 4 * here.index(core)
+    assert 8 * len(here) == 32 and 8 * len(there) == 32 and len({topo.chip(c) for c in there}) == 1
+    slot = 8 * here.index(core)
 
     def server(dst, group):
         gws = [x for x in group if topo.may_write(x, dst)]
@@ -89,173 +84,145 @@ def rank_program(g, core, T, topo):
                                                   dsts=[dst_ap] * len(dsts), alu_op=0)], local_sem=S.snt)
         sent[0] += bits(m)
 
-    nv = [0]
+    n_hl = bits(topo.mask(left, core))
+    n_hr = bits(topo.mask(via((rank + 1) % n), core))
+    n_ls = sum(bits(topo.mask(c, core)) for c in here if c != core)
+    n_rs = bits(topo.mask(server(core, there), core))
 
-    def dep(new):
-        if new and nv[0]:
-            vq.wait_ge(S.v, nv[0])
+    nv, na = [0], [0]
 
-    def done(ins):
+    def V(ins):
         ins.then_inc(S.v, 1)
         nv[0] += 1
         return nv[0]
 
-    def fill(ap, c):
-        return done(vq.memset(ap, c))
+    def A(ins):
+        ins.then_inc(S.a, 1)
+        na[0] += 1
+        return na[0]
 
-    def tt(out, a, b, op, new=True):
-        dep(new)
-        return done(vq.tensor_tensor(out, a, b, op))
+    def tt(out, x, y, op=ADD):
+        return V(vq.tensor_tensor(out, x, y, op))
 
-    def cp(out, a, new=True):
-        dep(new)
-        return done(vq.tensor_copy(out, a))
+    def amax(out, x):
+        return V(vq.tensor_reduce(out, x, AxisListType.X, MAX, apply_absolute_value=True))
 
-    wp = [0]
+    g.sync.dma_start(UX[:, 260:516], T.u[:, 256:512]).then_inc(S.ld_u1, 16)
+    aq.dma_start(UX[:, 4:260], T.u[:, 0:256]).then_inc(S.ld_u2, 16)
+    g.sync.dma_start(BX[:, 260:516], T.b[:, 256:512]).then_inc(S.ld_b1, 16)
+    aq.dma_start(BX[:, 4:260], T.b[:, 0:256]).then_inc(S.ld_b2, 16)
 
-    def wk(k):
-        a = wp[0]
-        wp[0] += k
-        return a
+    a_PU1, a_PU2, a_PB1, a_PB2, a_Y1, a_Y2, a_PSu, a_PSb, a_SQ1, a_SQ2, a_SQS, a_mean = range(1, 13)
 
-    def W(o, k):
-        return T.Wk[:, o:o + k]
-
-    def halve(o, width, op, stop):
-        while width > stop:
-            width //= 2
-            o2 = wk(width)
-            tt(W(o2, width), W(o, width), W(o + width, width), op)
-            o = o2
-        return o
-
-    vq.memset(T.Za[:, 1:129], 0.0).then_inc(S.za, 1)
-    vq.memset(T.Za[:, 0:1], -8.0).then_inc(S.za, 1)
-    vq.memset(T.Zb[:, 1:129], 0.0).then_inc(S.zb, 1)
-    vq.memset(T.Zb[:, 0:1], 4.0).then_inc(S.zb, 1)
-    fill(T.PC[:, 0:256], -1.0)
-    fill(T.PC[:, 256:512], 0.125)
-    fill(T.ONE[:, :], 1.0)
-    fill(T.LS[:, slot + 2:slot + 4], 0.0)
-    fill(T.FC[:, 0:1], 2.0 ** -21)
-    fill(T.FC[:, 1:2], 0.125)
-
-    g.sync.dma_start(T.UX[:, 6:518], T.u[:, :]).then_inc(S.ld_u, 16)
-    g.sync.wait_ge(S.zb, 2)
-    g.sync.dma_start(T.Db[:], T.Zb[:, :]).then_inc(S.db, 16)
-    g.sync.wait_ge(S.db, 16)
-    g.sync.dma_start(T.P4[:, :], T.Db[0:128 * 128]).then_inc(S.ib, 16)
-    g.scalar.dma_start(T.Bb[:, :], T.b[:, :]).then_inc(S.ld_b, 16)
-    g.scalar.wait_ge(S.za, 2)
-    g.scalar.dma_start(T.Da[:], T.Za[:, :]).then_inc(S.da, 16)
-    g.scalar.wait_ge(S.da, 16)
-    g.scalar.dma_start(T.M8[:, :], T.Da[0:128 * 128]).then_inc(S.ia, 16)
-
-    n_hl = bits(topo.mask(left, core))
-    se, x1, t1 = wk(8), wk(256), wk(256)
-    vq.wait_ge(S.ld_u, 16)
-    tt(T.S1[:, 0:511], T.UX[:, 6:517], T.UX[:, 7:518], ADD)
-    tt(T.Q[:, 0:508], T.S1[:, 0:508], T.S1[:, 3:511], ADD)
-    vq.wait_ge(S.aL, 2)
-    tt(T.E[:, 0:256], T.PAL[:, 2:258], T.Q[:, 0:256], ADD)
+    V(vq.memset(T.CF[:, 0:31], 1.0))
+    V(vq.memset(T.CF[:, 31:32], 0.125))
+    v_fill = V(vq.memset(ST[:, slot + 6:slot + 8], 0.0))
+    vq.wait_ge(S.ld_u1, 16)
+    v_Z1 = tt(Z[:, 260:515], UX[:, 260:515], UX[:, 261:516])
+    vq.wait_ge(S.ld_u2, 16)
+    v_Z2 = tt(Z[:, 4:260], UX[:, 4:260], UX[:, 5:261])
+    vq.wait_ge(S.v, v_Z1)
+    v_Q1 = tt(Q[:, 260:512], Z[:, 260:512], Z[:, 263:515])
+    vq.wait_ge(S.v, v_Z2)
+    v_Q2 = tt(Q[:, 4:260], Z[:, 4:260], Z[:, 7:263])
+    vq.wait_ge(S.v, v_Q1)
+    vq.wait_ge(S.a, a_PB1)
+    v_G1 = tt(G[:, 260:512], T.PB1[:, 0:252], Q[:, 260:512])
+    vq.wait_ge(S.v, v_Q2)
+    vq.wait_ge(S.a, a_PB2)
+    v_G2 = tt(G[:, 4:260], T.PB2[:, 0:256], Q[:, 4:260])
+    vq.wait_ge(S.v, v_G1)
+    v_E1 = tt(E[:, 260:512], T.PU1[:, 0:252], G[:, 260:512])
+    vq.wait_ge(S.v, v_G2)
+    v_E2 = tt(E[:, 4:260], T.PU2[:, 0:256], G[:, 4:260])
     vq.wait_ge(S.hu, n_hl)
-    tt(W(se, 7), T.UX[:, 2:9], T.UX[:, 3:10], ADD, new=False)
-    tt(T.PN[:, 0:256], T.PC[:, 0:256], T.E[:, 0:256], MUL)
-    tt(T.Q[:, 508:512], W(se, 4), W(se + 3, 4), ADD, new=False)
-    tt(T.SQ[:, 0:256], T.PN[:, 0:256], T.E[:, 0:256], MUL)
-    tt(T.PT[:, 0:256], T.PN[:, 0:256], T.E[:, 0:256], MAX, new=False)
-    tt(T.E[:, 510:512], T.PAL[:, 0:2], T.Q[:, 510:512], ADD, new=False)
-    vq.wait_ge(S.aR, 4)
-    n_sql = tt(T.E[:, 256:510], T.PAR[:, 0:254], T.Q[:, 256:510], ADD, new=False)
-    tt(T.PN[:, 256:512], T.PC[:, 0:256], T.E[:, 256:512], MUL)
-    tt(W(x1, 256), T.PT[:, 0:256], T.E[:, 256:512], MAX, new=False)
-    tt(T.SQ[:, 256:512], T.PN[:, 256:512], T.E[:, 256:512], MUL)
-    n_sqr = tt(W(t1, 256), T.PN[:, 256:512], W(x1, 256), MAX, new=False)
-    m16 = halve(t1, 256, MAX, 16)
-    vq.wait_ge(S.sm, 4)
-    n_ts = cp(T.TS[:, :], T.PS[:, 0:128], new=False)
-    m2 = halve(m16, 16, MAX, 2)
-    tt(T.LS[:, slot + 1:slot + 2], W(m2, 1), W(m2 + 1, 1), MAX)
-    vq.wait_ge(S.sm, 5)
-    n_part = cp(T.LS[:, slot:slot + 1], T.PS[:, 128:129], new=False)
-
-    tt(T.PN[:, 0:256], T.PC[:, 256:512], T.E[:, 0:256], MUL)
-    tt(T.PN[:, 256:512], T.PC[:, 256:512], T.E[:, 256:512], MUL, new=False)
-    tt(T.Y[:, 2:258], T.PN[:, 0:256], T.UX[:, 8:264], ADD)
-    tt(T.Y[:, 258:510], T.PN[:, 256:508], T.UX[:, 264:516], ADD, new=False)
-    tt(T.Y[:, 0:2], T.PN[:, 510:512], T.UX[:, 6:8], ADD, new=False)
-    sr, qr, er = wk(8), wk(2), wk(2)
-    vq.wait_ge(S.hr, bits(topo.mask(via((rank + 1) % n), core)))
-    tt(W(sr, 5), T.UX[:, 514:519], T.UX[:, 515:520], ADD, new=False)
-    tt(W(qr, 2), W(sr, 2), W(sr + 3, 2), ADD)
-    vq.wait_ge(S.ae, 2)
-    tt(W(er, 2), T.PE[:, 0:2], W(qr, 2), ADD)
-    tt(T.PN[:, 0:2], T.PC[:, 256:258], W(er, 2), MUL)
-    n_y = tt(T.Y[:, 510:512], T.PN[:, 0:2], T.UX[:, 516:518], ADD)
-
-    n_ls = sum(bits(topo.mask(c, core)) for c in here if c != core)
-    la, lm, la2, lm2 = wk(8), wk(8), wk(4), wk(4)
+    v_S1 = tt(Z[:, 0:4], UX[:, 0:4], UX[:, 1:5])
+    vq.wait_ge(S.v, v_E1)
+    amax(ST[:, slot + 1:slot + 2], E[:, 260:512])
+    vq.wait_ge(S.v, v_S1)
+    vq.wait_ge(S.a, a_PSb)
+    tt(T.A1[:, :], T.PSm[:, 4:8], Z[:, 0:4])
+    v_S2 = tt(T.A2[:, :], T.PSm[:, 0:4], Z[:, 3:7])
+    amax(ST[:, slot + 3:slot + 4], E[:, 4:260])
+    vq.wait_ge(S.v, v_S2)
+    v_S3 = tt(E[:, 0:4], T.A1[:, :], T.A2[:, :])
+    vq.wait_ge(S.v, v_S3)
+    v_part = amax(ST[:, slot + 5:slot + 6], E[:, 0:4])
+    V(vq.tensor_scalar(T.Y01[:, 0:1], E[:, 2:3], 0.125, UX[:, 4:5], MUL, ADD))
+    v_y01 = V(vq.tensor_scalar(T.Y01[:, 1:2], E[:, 3:4], 0.125, UX[:, 5:6], MUL, ADD))
+    v_GT = tt(T.GT[:, :], T.PB1[:, 252:254], Z[:, 512:514])
+    vq.wait_ge(S.hr, n_hr)
+    v_ZT = tt(T.ZT[:, :], UX[:, 515:517], UX[:, 516:518])
+    vq.wait_ge(S.v, v_ZT)
+    V(vq.tensor_scalar(T.YT[:, 0:1], T.ZT[:, 0:1], T.GT[:, 0:1], 0.125, ADD, MUL))
+    v_yt = V(vq.tensor_scalar(T.YT[:, 1:2], T.ZT[:, 1:2], T.GT[:, 1:2], 0.125, ADD, MUL))
     vq.wait_ge(S.ls, n_ls)
-    tt(W(la, 8), T.LS[:, 0:8], T.LS[:, 8:16], ADD)
-    tt(W(lm, 8), T.LS[:, 0:8], T.LS[:, 8:16], MAX, new=False)
-    tt(W(la2, 4), W(la, 4), W(la + 4, 4), ADD)
-    tt(W(lm2, 4), W(lm, 4), W(lm + 4, 4), MAX, new=False)
-    ra, rm, ra2, rm2 = wk(8), wk(8), wk(4), wk(4)
-    vq.wait_ge(S.rs, bits(topo.mask(server(core, there), core)))
-    tt(W(ra, 8), T.RS[:, 0:8], T.RS[:, 8:16], ADD)
-    tt(W(rm, 8), T.RS[:, 0:8], T.RS[:, 8:16], MAX, new=False)
-    tt(W(ra2, 4), W(ra, 4), W(ra + 4, 4), ADD)
-    tt(W(rm2, 4), W(rm, 4), W(rm + 4, 4), MAX, new=False)
-    tt(T.F[:, 0:1], W(ra2, 1), W(la2, 1), ADD)
-    tt(T.F[:, 1:2], W(rm2 + 1, 1), W(lm2 + 1, 1), MAX, new=False)
-    n_s = tt(T.SS[:, :], T.F[:, :], T.FC[:, :], MUL)
+    vq.wait_ge(S.rs, n_rs)
+    v_max = V(vq.tensor_tensor_scan(T.FB[:, 1:64:2], ST[:, 1:64:2], T.CF[:, :], 0.0, MAX, MUL))
 
-    pe.wait_ge(S.ia, 16)
-    pe.wait_ge(S.ld_u, 16)
-    pe.matmul(T.PAL[:, 0:258], M8, T.UX[:, 6:264], True, False).then_inc(S.aL, 1)
-    pe.wait_ge(S.ib, 16)
-    pe.wait_ge(S.ld_b, 16)
-    pe.matmul(T.PAL[:, 0:258], P4, T.Bb[:, 0:258], False, True).then_inc(S.aL, 1)
-    pe.matmul(T.PAR[:, 0:252], M8, T.UX[:, 264:516], True, False).then_inc(S.aR, 1)
-    pe.matmul(T.PAR[:, 0:252], P4, T.Bb[:, 258:510], False, True).then_inc(S.aR, 1)
-    pe.wait_ge(S.hu, n_hl)
-    pe.matmul(T.PAR[:, 252:254], M8, T.UX[:, 4:6], True, False).then_inc(S.aR, 1)
-    pe.wait_ge(S.hb, n_hl)
-    pe.matmul(T.PAR[:, 252:254], P4, T.UX[:, 0:2], False, True).then_inc(S.aR, 1)
-    pe.wait_ge(S.v, n_sql)
-    for k in range(4):
-        if k == 2:
-            pe.wait_ge(S.v, n_sqr)
-        pe.matmul(T.PS[:, 0:128], T.SQ[:, 128 * k:128 * k + 128], M8, k == 0, k == 3).then_inc(S.sm, 1)
-    pe.wait_ge(S.v, n_ts)
-    pe.matmul(T.PS[:, 128:129], T.TS[:, :], T.ONE[:, :], True, True).then_inc(S.sm, 1)
-    pe.matmul(T.PE[:, 0:2], M8, T.UX[:, 516:518], True, False).then_inc(S.ae, 1)
-    pe.matmul(T.PE[:, 0:2], P4, T.Bb[:, 510:512], False, True).then_inc(S.ae, 1)
+    def act(out, x, func, scale, acc=None):
+        return A(aq.activation(out, x, func, scale=scale, accum_out=acc))
 
-    g.wait_ge(S.ld_u, 16)
-    send(T.UX[:, 514:518], T.UX[:, 2:6], [right], S.hu)
-    g.wait_ge(S.ld_b, 16)
-    send(T.Bb[:, 510:512], T.UX[:, 0:2], [right], S.hb)
+    aq.wait_ge(S.ld_u1, 16)
+    assert act(T.PU1[:, 0:252], UX[:, 262:514], COPY, -8.0) == a_PU1
+    aq.wait_ge(S.ld_u2, 16)
+    assert act(T.PU2[:, 0:256], UX[:, 6:262], COPY, -8.0) == a_PU2
+    aq.wait_ge(S.ld_b1, 16)
+    assert act(T.PB1[:, 0:254], BX[:, 262:516], COPY, 4.0) == a_PB1
+    aq.wait_ge(S.ld_b2, 16)
+    assert act(T.PB2[:, 0:256], BX[:, 6:262], COPY, 4.0) == a_PB2
+    aq.wait_ge(S.v, v_G1)
+    assert act(T.Y[:, 258:510], G[:, 260:512], COPY, 0.125) == a_Y1
+    aq.wait_ge(S.v, v_G2)
+    assert act(T.Y[:, 2:258], G[:, 4:260], COPY, 0.125) == a_Y2
+    aq.wait_ge(S.hu, n_hl)
+    assert act(T.PSm[:, 0:4], UX[:, 2:6], COPY, -8.0) == a_PSu
+    aq.wait_ge(S.hb, n_hl)
+    assert act(T.PSm[:, 4:8], BX[:, 2:6], COPY, 4.0) == a_PSb
+    aq.wait_ge(S.v, v_E1)
+    assert act(T.J[:, 260:512], E[:, 260:512], SQUARE, 0.125, ST[:, slot:slot + 1]) == a_SQ1
+    aq.wait_ge(S.v, v_E2)
+    assert act(T.J[:, 4:260], E[:, 4:260], SQUARE, 0.125, ST[:, slot + 2:slot + 3]) == a_SQ2
+    aq.wait_ge(S.v, v_S3)
+    assert act(T.J[:, 0:4], E[:, 0:4], SQUARE, 0.125, ST[:, slot + 4:slot + 5]) == a_SQS
+    aq.wait_ge(S.a, a_SQS)
+    aq.wait_ge(S.ls, n_ls)
+    aq.wait_ge(S.rs, n_rs)
+    assert act(T.J2[:, :], ST[:, 0:64:2], COPY, 2.0 ** -12, T.FB[:, 62:63]) == a_mean
+
+    g.wait_ge(S.ld_u1, 16)
+    send(UX[:, 512:516], UX[:, 0:4], [right], S.hu)
+    g.wait_ge(S.ld_u2, 16)
     carrier = via(rank)
     if carrier == core:
-        send(T.UX[:, 6:8], T.UX[:, 518:520], [left], S.hr)
+        send(UX[:, 4:6], UX[:, 516:518], [left], S.hr)
     else:
-        send(T.UX[:, 6:8], T.RL[:, 2 * rank:2 * rank + 2], [carrier], S.rl)
+        send(UX[:, 4:6], T.RL[:, 2 * rank:2 * rank + 2], [carrier], S.rl)
+    g.wait_ge(S.ld_b1, 16)
+    send(BX[:, 514:516], BX[:, 2:4], [right], S.hb)
     pass_on = [i for i in range(n) if i != rank and via(i) == core]
     if pass_on:
         g.wait_ge(S.rl, sum(bits(topo.mask(cores[i], core)) for i in pass_on))
         for i in pass_on:
-            send(T.RL[:, 2 * i:2 * i + 2], T.UX[:, 518:520], [cores[(i - 1) % n]], S.hr)
-    g.wait_ge(S.v, n_part)
+            send(T.RL[:, 2 * i:2 * i + 2], UX[:, 516:518], [cores[(i - 1) % n]], S.hr)
+    g.wait_ge(S.v, v_part)
+    g.wait_ge(S.a, a_SQS)
     others = [c for c in gates if c != core] + [c for c in here if c != core and c not in gates]
-    send(T.LS[:, slot:slot + 4], T.LS[:, slot:slot + 4], others, S.ls)
+    send(ST[:, slot:slot + 8], ST[:, slot:slot + 8], others, S.ls)
     if serve:
         g.wait_ge(S.ls, n_ls)
-        send(T.LS[:, 0:16], T.RS[:, 0:16], serve, S.rs)
+        send(ST[:, 0:32], ST[:, 32:64], serve, S.rs)
     g.wait_ge(S.snt, sent[0])
 
-    g.sync.wait_ge(S.v, n_y)
-    g.sync.dma_start(T.y[:, :], T.Y[:, :]).then_inc(S.st, 16)
-    g.sync.wait_ge(S.v, n_s)
-    g.sync.dma_start(T.s[:, :], T.SS[:, :]).then_inc(S.st, 16)
-    g.sync.wait_ge(S.st, 32)
+    g.sync.wait_ge(S.a, a_Y1)
+    g.sync.dma_start(T.y[:, 258:510], T.Y[:, 258:510]).then_inc(S.st, 16)
+    g.sync.wait_ge(S.a, a_Y2)
+    g.sync.dma_start(T.y[:, 2:258], T.Y[:, 2:258]).then_inc(S.st, 16)
+    g.sync.wait_ge(S.v, v_y01)
+    g.sync.dma_start(T.y[:, 0:2], T.Y01[:, :]).then_inc(S.st, 16)
+    g.sync.wait_ge(S.v, v_yt)
+    g.sync.dma_start(T.y[:, 510:512], T.YT[:, :]).then_inc(S.st, 16)
+    g.sync.wait_ge(S.v, v_max)
+    g.sync.wait_ge(S.a, a_mean)
+    g.sync.dma_start(T.s[:, :], T.FB[:, 62:64]).then_inc(S.st, 16)
+    g.sync.wait_ge(S.st, 80)

from concourse.bass import DstId, RemoteDMATransfer
from concourse.mybir import AluOpType, AxisListType, ActivationFunctionType

F32 = "float32"
SCRATCH = {
    "UX": ("sbuf", [128, 520], F32),
    "BX": ("sbuf", [128, 516], F32),
    "RL": ("sbuf", [128, 16], F32),
    "Z": ("sbuf", [128, 516], F32),
    "Q": ("sbuf", [128, 512], F32),
    "G": ("sbuf", [128, 512], F32),
    "E": ("sbuf", [128, 512], F32),
    "J": ("sbuf", [128, 512], F32),
    "J2": ("sbuf", [128, 32], F32),
    "Y": ("sbuf", [128, 512], F32),
    "Y01": ("sbuf", [128, 2], F32),
    "YT": ("sbuf", [128, 2], F32),
    "A1": ("sbuf", [128, 4], F32),
    "A2": ("sbuf", [128, 4], F32),
    "GT": ("sbuf", [128, 2], F32),
    "ZT": ("sbuf", [128, 2], F32),
    "ST": ("sbuf", [128, 64], F32),
    "CF": ("sbuf", [128, 32], F32),
    "FB": ("sbuf", [128, 64], F32),
    "PU1": ("psum", [128, 512], F32),
    "PU2": ("psum", [128, 512], F32),
    "PB1": ("psum", [128, 512], F32),
    "PB2": ("psum", [128, 512], F32),
    "PSm": ("psum", [128, 512], F32),
}
SEMAPHORES = ["v", "a", "ld_u1", "ld_u2", "ld_b1", "ld_b2", "hu", "hb", "hr", "rl", "ls", "rs", "snt", "st"]


def rank_program(g, core, T, topo):
    rank = T.rank_of(core)
    if rank is None:
        return
    cores = list(T.cores)
    n = len(cores)
    S = T.sem
    ADD, MUL, MAX = AluOpType.add, AluOpType.mult, AluOpType.max
    COPY, SQUARE = ActivationFunctionType.Copy, ActivationFunctionType.Square
    vq, aq = g.vector, g.scalar
    UX, BX, Z, Q, G, E, ST = T.UX, T.BX, T.Z, T.Q, T.G, T.E, T.ST

    def bits(m):
        return bin(m).count("1")

    right, left = cores[(rank + 1) % n], cores[(rank - 1) % n]
    for i in range(n):
        assert topo.may_write(cores[i], cores[(i + 1) % n])

    def via(i):
        src, dst = cores[i], cores[(i - 1) % n]
        if topo.may_write(src, dst):
            return src
        return [x for x in cores if x != src and topo.chip(x) == topo.chip(src) and topo.may_write(x, dst)][0]

    here = [c for c in cores if topo.chip(c) == topo.chip(core)]
    there = [c for c in cores if topo.chip(c) != topo.chip(core)]
    assert 8 * len(here) == 32 and 8 * len(there) == 32 and len({topo.chip(c) for c in there}) == 1
    slot = 8 * here.index(core)

    def server(dst, group):
        gws = [x for x in group if topo.may_write(x, dst)]
        same = [x for x in gws if topo.die(x) == topo.die(dst)]
        return (same or gws)[0]

    serve = [d for d in there if server(d, here) == core]
    gates = [x for x in here if any(server(d, here) == x for d in there)]

    sent = [0]

    def send(src_ap, dst_ap, dsts, sem):
        m = topo.mask(core, dsts[0])
        for d in dsts:
            m &= topo.mask(core, d)
        if len(dsts) == 1:
            rid, pid, _ = topo.addr(dsts[0])
            g.remote_dma(dst_ap, src_ap, sem, S.snt, pid, rid, m)
        else:
            ids = [DstId(rid=topo.addr(d)[0], pnc=topo.addr(d)[1]) for d in dsts]
            g.remote_dma_fused([RemoteDMATransfer(dst_ids=ids, dma_engine_mask=m, remote_sem=sem, srcs=[src_ap],
                                                  dsts=[dst_ap] * len(dsts), alu_op=0)], local_sem=S.snt)
        sent[0] += bits(m)

    n_hl = bits(topo.mask(left, core))
    n_hr = bits(topo.mask(via((rank + 1) % n), core))
    n_ls = sum(bits(topo.mask(c, core)) for c in here if c != core)
    n_rs = bits(topo.mask(server(core, there), core))

    nv, na = [0], [0]

    def V(ins):
        ins.then_inc(S.v, 1)
        nv[0] += 1
        return nv[0]

    def A(ins):
        ins.then_inc(S.a, 1)
        na[0] += 1
        return na[0]

    def tt(out, x, y, op=ADD):
        return V(vq.tensor_tensor(out, x, y, op))

    def amax(out, x):
        return V(vq.tensor_reduce(out, x, AxisListType.X, MAX, apply_absolute_value=True))

    g.sync.dma_start(UX[:, 260:516], T.u[:, 256:512]).then_inc(S.ld_u1, 16)
    aq.dma_start(UX[:, 4:260], T.u[:, 0:256]).then_inc(S.ld_u2, 16)
    g.sync.dma_start(BX[:, 260:516], T.b[:, 256:512]).then_inc(S.ld_b1, 16)
    aq.dma_start(BX[:, 4:260], T.b[:, 0:256]).then_inc(S.ld_b2, 16)

    a_PU1, a_PU2, a_PB1, a_PB2, a_Y1, a_Y2, a_PSu, a_PSb, a_SQ1, a_SQ2, a_SQS, a_mean = range(1, 13)

    V(vq.memset(T.CF[:, 0:31], 1.0))
    V(vq.memset(T.CF[:, 31:32], 0.125))
    v_fill = V(vq.memset(ST[:, slot + 6:slot + 8], 0.0))
    vq.wait_ge(S.ld_u1, 16)
    v_Z1 = tt(Z[:, 260:515], UX[:, 260:515], UX[:, 261:516])
    vq.wait_ge(S.ld_u2, 16)
    v_Z2 = tt(Z[:, 4:260], UX[:, 4:260], UX[:, 5:261])
    vq.wait_ge(S.v, v_Z1)
    v_Q1 = tt(Q[:, 260:512], Z[:, 260:512], Z[:, 263:515])
    vq.wait_ge(S.v, v_Z2)
    v_Q2 = tt(Q[:, 4:260], Z[:, 4:260], Z[:, 7:263])
    vq.wait_ge(S.v, v_Q1)
    vq.wait_ge(S.a, a_PB1)
    v_G1 = tt(G[:, 260:512], T.PB1[:, 0:252], Q[:, 260:512])
    vq.wait_ge(S.v, v_Q2)
    vq.wait_ge(S.a, a_PB2)
    v_G2 = tt(G[:, 4:260], T.PB2[:, 0:256], Q[:, 4:260])
    vq.wait_ge(S.v, v_G1)
    v_E1 = tt(E[:, 260:512], T.PU1[:, 0:252], G[:, 260:512])
    vq.wait_ge(S.v, v_G2)
    v_E2 = tt(E[:, 4:260], T.PU2[:, 0:256], G[:, 4:260])
    vq.wait_ge(S.hu, n_hl)
    v_S1 = tt(Z[:, 0:4], UX[:, 0:4], UX[:, 1:5])
    vq.wait_ge(S.v, v_E1)
    amax(ST[:, slot + 1:slot + 2], E[:, 260:512])
    vq.wait_ge(S.v, v_S1)
    vq.wait_ge(S.a, a_PSb)
    tt(T.A1[:, :], T.PSm[:, 4:8], Z[:, 0:4])
    v_S2 = tt(T.A2[:, :], T.PSm[:, 0:4], Z[:, 3:7])
    amax(ST[:, slot + 3:slot + 4], E[:, 4:260])
    vq.wait_ge(S.v, v_S2)
    v_S3 = tt(E[:, 0:4], T.A1[:, :], T.A2[:, :])
    vq.wait_ge(S.v, v_S3)
    v_part = amax(ST[:, slot + 5:slot + 6], E[:, 0:4])
    V(vq.tensor_scalar(T.Y01[:, 0:1], E[:, 2:3], 0.125, UX[:, 4:5], MUL, ADD))
    v_y01 = V(vq.tensor_scalar(T.Y01[:, 1:2], E[:, 3:4], 0.125, UX[:, 5:6], MUL, ADD))
    v_GT = tt(T.GT[:, :], T.PB1[:, 252:254], Z[:, 512:514])
    vq.wait_ge(S.hr, n_hr)
    v_ZT = tt(T.ZT[:, :], UX[:, 515:517], UX[:, 516:518])
    vq.wait_ge(S.v, v_ZT)
    V(vq.tensor_scalar(T.YT[:, 0:1], T.ZT[:, 0:1], T.GT[:, 0:1], 0.125, ADD, MUL))
    v_yt = V(vq.tensor_scalar(T.YT[:, 1:2], T.ZT[:, 1:2], T.GT[:, 1:2], 0.125, ADD, MUL))
    vq.wait_ge(S.ls, n_ls)
    vq.wait_ge(S.rs, n_rs)
    v_max = V(vq.tensor_tensor_scan(T.FB[:, 1:64:2], ST[:, 1:64:2], T.CF[:, :], 0.0, MAX, MUL))

    def act(out, x, func, scale, acc=None):
        return A(aq.activation(out, x, func, scale=scale, accum_out=acc))

    aq.wait_ge(S.ld_u1, 16)
    assert act(T.PU1[:, 0:252], UX[:, 262:514], COPY, -8.0) == a_PU1
    aq.wait_ge(S.ld_u2, 16)
    assert act(T.PU2[:, 0:256], UX[:, 6:262], COPY, -8.0) == a_PU2
    aq.wait_ge(S.ld_b1, 16)
    assert act(T.PB1[:, 0:254], BX[:, 262:516], COPY, 4.0) == a_PB1
    aq.wait_ge(S.ld_b2, 16)
    assert act(T.PB2[:, 0:256], BX[:, 6:262], COPY, 4.0) == a_PB2
    aq.wait_ge(S.v, v_G1)
    assert act(T.Y[:, 258:510], G[:, 260:512], COPY, 0.125) == a_Y1
    aq.wait_ge(S.v, v_G2)
    assert act(T.Y[:, 2:258], G[:, 4:260], COPY, 0.125) == a_Y2
    aq.wait_ge(S.hu, n_hl)
    assert act(T.PSm[:, 0:4], UX[:, 2:6], COPY, -8.0) == a_PSu
    aq.wait_ge(S.hb, n_hl)
    assert act(T.PSm[:, 4:8], BX[:, 2:6], COPY, 4.0) == a_PSb
    aq.wait_ge(S.v, v_E1)
    assert act(T.J[:, 260:512], E[:, 260:512], SQUARE, 0.125, ST[:, slot:slot + 1]) == a_SQ1
    aq.wait_ge(S.v, v_E2)
    assert act(T.J[:, 4:260], E[:, 4:260], SQUARE, 0.125, ST[:, slot + 2:slot + 3]) == a_SQ2
    aq.wait_ge(S.v, v_S3)
    assert act(T.J[:, 0:4], E[:, 0:4], SQUARE, 0.125, ST[:, slot + 4:slot + 5]) == a_SQS
    aq.wait_ge(S.a, a_SQS)
    aq.wait_ge(S.ls, n_ls)
    aq.wait_ge(S.rs, n_rs)
    assert act(T.J2[:, :], ST[:, 0:64:2], COPY, 2.0 ** -12, T.FB[:, 62:63]) == a_mean

    g.wait_ge(S.ld_u1, 16)
    send(UX[:, 512:516], UX[:, 0:4], [right], S.hu)
    g.wait_ge(S.ld_u2, 16)
    carrier = via(rank)
    if carrier == core:
        send(UX[:, 4:6], UX[:, 516:518], [left], S.hr)
    else:
        send(UX[:, 4:6], T.RL[:, 2 * rank:2 * rank + 2], [carrier], S.rl)
    g.wait_ge(S.ld_b1, 16)
    send(BX[:, 514:516], BX[:, 2:4], [right], S.hb)
    pass_on = [i for i in range(n) if i != rank and via(i) == core]
    if pass_on:
        g.wait_ge(S.rl, sum(bits(topo.mask(cores[i], core)) for i in pass_on))
        for i in pass_on:
            send(T.RL[:, 2 * i:2 * i + 2], UX[:, 516:518], [cores[(i - 1) % n]], S.hr)
    g.wait_ge(S.v, v_part)
    g.wait_ge(S.a, a_SQS)
    others = [c for c in gates if c != core] + [c for c in here if c != core and c not in gates]
    send(ST[:, slot:slot + 8], ST[:, slot:slot + 8], others, S.ls)
    if serve:
        g.wait_ge(S.ls, n_ls)
        send(ST[:, 0:32], ST[:, 32:64], serve, S.rs)
    g.wait_ge(S.snt, sent[0])

    g.sync.wait_ge(S.a, a_Y1)
    g.sync.dma_start(T.y[:, 258:510], T.Y[:, 258:510]).then_inc(S.st, 16)
    g.sync.wait_ge(S.a, a_Y2)
    g.sync.dma_start(T.y[:, 2:258], T.Y[:, 2:258]).then_inc(S.st, 16)
    g.sync.wait_ge(S.v, v_y01)
    g.sync.dma_start(T.y[:, 0:2], T.Y01[:, :]).then_inc(S.st, 16)
    g.sync.wait_ge(S.v, v_yt)
    g.sync.dma_start(T.y[:, 510:512], T.YT[:, :]).then_inc(S.st, 16)
    g.sync.wait_ge(S.v, v_max)
    g.sync.wait_ge(S.a, a_mean)
    g.sync.dma_start(T.s[:, :], T.FB[:, 62:64]).then_inc(S.st, 16)
    g.sync.wait_ge(S.st, 80)
